import numpy as np, ml_dtypes
CORES = [22,46,70,150,174,198,278,302,326,406,430,454]
N = 12
import mx_ref
NC, KT = 256, 1
FROM = [11,7,6,1,8,4,10,9,3,5,0,2]
BF = ml_dtypes.bfloat16
def setup_inputs(rng):
    def f(*shape):
        return mx_ref.flush((rng.standard_normal(shape, dtype=np.float32) * np.exp2(rng.integers(-2, 3, shape[:-1] + (1,)))).astype(BF))
    return {"w": f(N, 128, KT * 512), "x": f(N, 128, KT * 4 * NC)}
def setup_inputs_blocks(rng):
    d = setup_inputs(rng)
    for k in ("w", "x"): d[k] = mx_ref.spread(d[k], rng, 4)
    return d
def setup_inputs_wide(rng):
    d = setup_inputs(rng)
    for k in ("w", "x"): d[k] = mx_ref.flush((d[k].astype(np.float32) * np.exp2(rng.integers(-8, 9, (N, 1, 1))).astype(np.float32)).astype(BF))
    return d
def setup_inputs_zeros(rng):
    d = setup_inputs(rng); v = d["x"].reshape(N, 128, -1, 4).copy()
    v[np.broadcast_to((rng.random((N, 1, v.shape[2], 1)) < 0.33), v.shape)] = 0
    d["x"] = v.reshape(d["x"].shape)
    return d
def reference(w, x):
    y = np.zeros((N, 128, NC), np.float32)
    for r in range(N):
        for t in range(KT):
            p = mx_ref.matmul(mx_ref.quantize(w[r][:, 512 * t:512 * t + 512]), mx_ref.quantize(x[FROM[r]][:, 4 * NC * t:4 * NC * t + 4 * NC]))
            y[r] = p if t == 0 else y[r] + p
    return {"y": y}

@@ -1,0 +1,108 @@
+from concourse.mybir import dt, ActivationFunctionType
+
+NC = 256
+H = NC // 2
+MW = 128
+
+SCRATCH = {
+    "xb": ("sbuf", [128, 4 * NC], "bfloat16"),
+    "wb": ("sbuf", [128, 4 * MW], "bfloat16"),
+    "xq": ("sbuf", [128, NC], "float8_e4m3fn_x4"),
+    "xs": ("sbuf", [128, NC], "uint8"),
+    "wq": ("sbuf", [128, MW], "float8_e4m3fn_x4"),
+    "ws": ("sbuf", [128, MW], "uint8"),
+    "lq": ("sbuf", [128, NC], "float8_e4m3fn_x4"),
+    "ls": ("sbuf", [128, NC], "uint8"),
+    "rq": ("sbuf", [128, NC], "float8_e4m3fn_x4"),
+    "rs": ("sbuf", [128, NC], "uint8"),
+    "yb": ("sbuf", [128, NC], "float32"),
+    "ps": ("psum", [128, 1024], "float32"),
+}
+SEMAPHORES = ["ldx", "ldw", "qx", "qw", "arr", "inq", "ins", "sent", "ma", "mb", "cv", "cs", "st"]
+
+
+def _one_link(topo, a, b):
+    if not topo.may_write(a, b):
+        return False
+    if topo.rack(topo.host(a)) == topo.rack(topo.host(b)):
+        return topo.same_plane(a, b) or topo.mates(a, b)
+    return topo.chip(a) == topo.chip(b)
+
+
+def _routes(T, topo):
+    cores, frm = T.cores, T.tables["FROM"]
+    routes = {}
+    for r, j in enumerate(frm):
+        src, dst = cores[j], cores[r]
+        if topo.may_write(src, dst):
+            routes[src] = ([dst], [dst])
+            continue
+        mids = [m for m in cores if m != src and m != dst and _one_link(topo, src, m) and _one_link(topo, m, dst)]
+        mids.sort(key=lambda m: topo.rack(topo.host(m)) == topo.rack(topo.host(src)))
+        routes[src] = ([mids[0], dst], [mids[-1], dst])
+    return routes
+
+
+def _engines(mask):
+    return bin(mask).count("1")
+
+
+def rank_program(g, core, T, topo):
+    if T.rank_of(core) is None:
+        return
+    S = T.sem
+    routes = _routes(T, topo)
+    sent = [0]
+
+    def write(kind, src_buf, dst, last):
+        rid, pid = topo.addr(dst, core)
+        mask = topo.mask(core, dst)
+        if kind == "q":
+            out = (T.lq if last else T.rq)[:].bitcast(dt.uint8)
+            in_ = src_buf[:].bitcast(dt.uint8)
+        else:
+            out = (T.ls if last else T.rs)[:]
+            in_ = src_buf[:]
+        sem = S.arr if last else (S.inq if kind == "q" else S.ins)
+        g.remote_dma(out_ap=out, in_ap=in_, remote_sem=sem, local_sem=S.sent, pid=pid, routing_id=rid,
+                     dma_engine_mask=mask)
+        sent[0] += _engines(mask)
+
+    g.sync.dma_start(T.xb[:], T.x[:]).then_inc(S.ldx, 16)
+    g.sync.dma_start(T.wb[:], T.w[:]).then_inc(S.ldw, 16)
+    g.vector.wait_ge(S.ldx, 16)
+    g.vector.quantize_mx(T.xq[:], T.xs[:], T.xb[:]).then_inc(S.qx, 1)
+    g.vector.wait_ge(S.ldw, 16)
+    g.vector.quantize_mx(T.wq[:], T.ws[:], T.wb[:]).then_inc(S.qw, 1)
+
+    way_q, way_s = routes[core]
+    g.wait_ge(S.qx, 1)
+    write("q", T.xq, way_q[0], len(way_q) == 1)
+    write("s", T.xs, way_s[0], len(way_s) == 1)
+
+    arrive = 0
+    for src, (wq_, ws_) in routes.items():
+        if len(wq_) == 2 and wq_[0] == core:
+            g.wait_ge(S.inq, _engines(topo.mask(src, core)))
+            write("q", T.rq, wq_[1], True)
+        if wq_[-1] == core:
+            arrive = _engines(topo.mask(([src] + wq_)[-2], core)) + _engines(topo.mask(([src] + ws_)[-2], core))
+    for src, (wq_, ws_) in routes.items():
+        if len(ws_) == 2 and ws_[0] == core:
+            g.wait_ge(S.ins, _engines(topo.mask(src, core)))
+            write("s", T.rs, ws_[1], True)
+
+    g.tensor.wait_ge(S.qw, 1)
+    g.tensor.wait_ge(S.arr, arrive)
+    g.tensor.matmul_mx(T.ps[:, 0:H], T.wq[:], T.ws[:], T.lq[:, 0:H], T.ls[:, 0:H], True, True).then_inc(S.ma, 1)
+    g.tensor.matmul_mx(T.ps[:, 512:512 + H], T.wq[:], T.ws[:], T.lq[:, H:NC], T.ls[:, H:NC], True, True).then_inc(S.mb, 1)
+    g.vector.wait_ge(S.ma, 1)
+    g.vector.tensor_copy(T.yb[:, 0:H], T.ps[:, 0:H]).then_inc(S.cv, 1)
+    g.scalar.wait_ge(S.mb, 1)
+    g.scalar.activation(T.yb[:, H:NC], T.ps[:, 512:512 + H], ActivationFunctionType.Copy).then_inc(S.cs, 1)
+
+    g.sync.wait_ge(S.cv, 1)
+    g.sync.wait_ge(S.cs, 1)
+    g.sync.dma_start(T.y[:], T.yb[:]).then_inc(S.st, 16)
+    g.sync.wait_ge(S.st, 16)
+    g.wait_ge(S.sent, sent[0])

@@ -1,3 +1,4 @@
+from concourse.bass import DstId, RemoteDMATransfer
 from concourse.mybir import dt, ActivationFunctionType
 
 NC = 256
@@ -18,7 +19,8 @@ SCRATCH = {
     "yb": ("sbuf", [128, NC], "float32"),
     "ps": ("psum", [128, 1024], "float32"),
 }
-SEMAPHORES = ["ldx", "ldw", "qx", "qw", "arr", "inq", "ins", "sent", "ma", "mb", "cv", "cs", "st"]
+SEMAPHORES = ["ld0", "ld1", "ldw", "q0", "q1", "qw", "arr0", "arr1", "inq0", "inq1", "ins", "sent",
+              "mm0", "mm1", "cp0", "cp1", "st"]
 
 
 def _one_link(topo, a, b):
@@ -35,16 +37,22 @@ def _routes(T, topo):
     for r, j in enumerate(frm):
         src, dst = cores[j], cores[r]
         if topo.may_write(src, dst):
-            routes[src] = ([dst], [dst])
+            routes[src] = (dst, dst, dst)
             continue
         mids = [m for m in cores if m != src and m != dst and _one_link(topo, src, m) and _one_link(topo, m, dst)]
         mids.sort(key=lambda m: topo.rack(topo.host(m)) == topo.rack(topo.host(src)))
-        routes[src] = ([mids[0], dst], [mids[-1], dst])
+        routes[src] = (dst, mids[0], mids[-1])
     return routes
 
 
 def _engines(mask):
     return bin(mask).count("1")
+
+
+def _halves(mask):
+    bits = [1 << i for i in range(16) if (mask >> i) & 1]
+    k = len(bits) // 2
+    return sum(bits[:k]), sum(bits[k:])
 
 
 def rank_program(g, core, T, topo):
@@ -54,55 +62,66 @@ def rank_program(g, core, T, topo):
     routes = _routes(T, topo)
     sent = [0]
 
-    def write(kind, src_buf, dst, last):
+    def cols(buf, h):
+        return buf[:, h * H:h * H + H]
+
+    def codes(h, src_buf, dst, last):
         rid, pid = topo.addr(dst, core)
         mask = topo.mask(core, dst)
-        if kind == "q":
-            out = (T.lq if last else T.rq)[:].bitcast(dt.uint8)
-            in_ = src_buf[:].bitcast(dt.uint8)
-        else:
-            out = (T.ls if last else T.rs)[:]
-            in_ = src_buf[:]
-        sem = S.arr if last else (S.inq if kind == "q" else S.ins)
-        g.remote_dma(out_ap=out, in_ap=in_, remote_sem=sem, local_sem=S.sent, pid=pid, routing_id=rid,
+        g.remote_dma(out_ap=cols(T.lq if last else T.rq, h).bitcast(dt.uint8), in_ap=cols(src_buf, h).bitcast(dt.uint8),
+                     remote_sem=S["arr%d" % h] if last else S["inq%d" % h], local_sem=S.sent, pid=pid, routing_id=rid,
                      dma_engine_mask=mask)
         sent[0] += _engines(mask)
 
-    g.sync.dma_start(T.xb[:], T.x[:]).then_inc(S.ldx, 16)
+    def plane(src_buf, dst, last):
+        rid, pid = topo.addr(dst, core)
+        masks = _halves(topo.mask(core, dst))
+        g.remote_dma_fused([RemoteDMATransfer(dst_ids=[DstId(rid=rid, pnc=pid)], dma_engine_mask=masks[h],
+                                              remote_sem=S["arr%d" % h] if last else S.ins,
+                                              src=cols(src_buf, h), dst=cols(T.ls if last else T.rs, h))
+                            for h in (0, 1)], local_sem=S.sent)
+        sent[0] += _engines(masks[0]) + _engines(masks[1])
+
+    for h in (0, 1):
+        g.sync.dma_start(T.xb[:, 4 * h * H:4 * (h + 1) * H], T.x[:, 4 * h * H:4 * (h + 1) * H]).then_inc(S["ld%d" % h], 16)
     g.sync.dma_start(T.wb[:], T.w[:]).then_inc(S.ldw, 16)
-    g.vector.wait_ge(S.ldx, 16)
-    g.vector.quantize_mx(T.xq[:], T.xs[:], T.xb[:]).then_inc(S.qx, 1)
+    for h in (0, 1):
+        g.vector.wait_ge(S["ld%d" % h], 16)
+        g.vector.quantize_mx(cols(T.xq, h), cols(T.xs, h), T.xb[:, 4 * h * H:4 * (h + 1) * H]).then_inc(S["q%d" % h], 1)
     g.vector.wait_ge(S.ldw, 16)
     g.vector.quantize_mx(T.wq[:], T.ws[:], T.wb[:]).then_inc(S.qw, 1)
 
-    way_q, way_s = routes[core]
-    g.wait_ge(S.qx, 1)
-    write("q", T.xq, way_q[0], len(way_q) == 1)
-    write("s", T.xs, way_s[0], len(way_s) == 1)
+    end, to_q, to_s = routes[core]
+    for h in (0, 1):
+        g.wait_ge(S["q%d" % h], 1)
+        codes(h, T.xq, to_q, to_q == end)
+    plane(T.xs, to_s, to_s == end)
 
-    arrive = 0
-    for src, (wq_, ws_) in routes.items():
-        if len(wq_) == 2 and wq_[0] == core:
-            g.wait_ge(S.inq, _engines(topo.mask(src, core)))
-            write("q", T.rq, wq_[1], True)
-        if wq_[-1] == core:
-            arrive = _engines(topo.mask(([src] + wq_)[-2], core)) + _engines(topo.mask(([src] + ws_)[-2], core))
-    for src, (wq_, ws_) in routes.items():
-        if len(ws_) == 2 and ws_[0] == core:
+    arrive = [0, 0]
+    for src, (dst, mid_q, mid_s) in routes.items():
+        if mid_q == core and dst != core:
+            for h in (0, 1):
+                g.wait_ge(S["inq%d" % h], _engines(topo.mask(src, core)))
+                codes(h, T.rq, dst, True)
+        if mid_s == core and dst != core:
             g.wait_ge(S.ins, _engines(topo.mask(src, core)))
-            write("s", T.rs, ws_[1], True)
+            plane(T.rs, dst, True)
+        if dst == core:
+            for h in (0, 1):
+                arrive[h] = (_engines(topo.mask(src if mid_q == dst else mid_q, core))
+                             + _engines(_halves(topo.mask(src if mid_s == dst else mid_s, core))[h]))
 
     g.tensor.wait_ge(S.qw, 1)
-    g.tensor.wait_ge(S.arr, arrive)
-    g.tensor.matmul_mx(T.ps[:, 0:H], T.wq[:], T.ws[:], T.lq[:, 0:H], T.ls[:, 0:H], True, True).then_inc(S.ma, 1)
-    g.tensor.matmul_mx(T.ps[:, 512:512 + H], T.wq[:], T.ws[:], T.lq[:, H:NC], T.ls[:, H:NC], True, True).then_inc(S.mb, 1)
-    g.vector.wait_ge(S.ma, 1)
-    g.vector.tensor_copy(T.yb[:, 0:H], T.ps[:, 0:H]).then_inc(S.cv, 1)
-    g.scalar.wait_ge(S.mb, 1)
-    g.scalar.activation(T.yb[:, H:NC], T.ps[:, 512:512 + H], ActivationFunctionType.Copy).then_inc(S.cs, 1)
-
-    g.sync.wait_ge(S.cv, 1)
-    g.sync.wait_ge(S.cs, 1)
-    g.sync.dma_start(T.y[:], T.yb[:]).then_inc(S.st, 16)
-    g.sync.wait_ge(S.st, 16)
+    for h in (0, 1):
+        g.tensor.wait_ge(S["arr%d" % h], arrive[h])
+        g.tensor.matmul_mx(T.ps[:, 512 * h:512 * h + H], T.wq[:], T.ws[:], cols(T.lq, h), cols(T.ls, h),
+                           True, True).then_inc(S["mm%d" % h], 1)
+    g.vector.wait_ge(S.mm0, 1)
+    g.vector.tensor_copy(cols(T.yb, 0), T.ps[:, 0:H]).then_inc(S.cp0, 1)
+    g.scalar.wait_ge(S.mm1, 1)
+    g.scalar.activation(cols(T.yb, 1), T.ps[:, 512:512 + H], ActivationFunctionType.Copy).then_inc(S.cp1, 1)
+    for h in (0, 1):
+        g.sync.wait_ge(S["cp%d" % h], 1)
+        g.sync.dma_start(cols(T.y, h), cols(T.yb, h)).then_inc(S.st, 16)
+    g.sync.wait_ge(S.st, 32)
     g.wait_ge(S.sent, sent[0])

from concourse.bass import DstId, RemoteDMATransfer
from concourse.mybir import dt, ActivationFunctionType

NC = 256
H = NC // 2
MW = 128

SCRATCH = {
    "xb": ("sbuf", [128, 4 * NC], "bfloat16"),
    "wb": ("sbuf", [128, 4 * MW], "bfloat16"),
    "xq": ("sbuf", [128, NC], "float8_e4m3fn_x4"),
    "xs": ("sbuf", [128, NC], "uint8"),
    "wq": ("sbuf", [128, MW], "float8_e4m3fn_x4"),
    "ws": ("sbuf", [128, MW], "uint8"),
    "lq": ("sbuf", [128, NC], "float8_e4m3fn_x4"),
    "ls": ("sbuf", [128, NC], "uint8"),
    "rq": ("sbuf", [128, NC], "float8_e4m3fn_x4"),
    "rs": ("sbuf", [128, NC], "uint8"),
    "yb": ("sbuf", [128, NC], "float32"),
    "ps": ("psum", [128, 1024], "float32"),
}
SEMAPHORES = ["ld0", "ld1", "ldw", "q0", "q1", "qw", "arr0", "arr1", "inq0", "inq1", "ins", "sent",
              "mm0", "mm1", "cp0", "cp1", "st"]


def _one_link(topo, a, b):
    if not topo.may_write(a, b):
        return False
    if topo.rack(topo.host(a)) == topo.rack(topo.host(b)):
        return topo.same_plane(a, b) or topo.mates(a, b)
    return topo.chip(a) == topo.chip(b)


def _routes(T, topo):
    cores, frm = T.cores, T.tables["FROM"]
    routes = {}
    for r, j in enumerate(frm):
        src, dst = cores[j], cores[r]
        if topo.may_write(src, dst):
            routes[src] = (dst, dst, dst)
            continue
        mids = [m for m in cores if m != src and m != dst and _one_link(topo, src, m) and _one_link(topo, m, dst)]
        mids.sort(key=lambda m: topo.rack(topo.host(m)) == topo.rack(topo.host(src)))
        routes[src] = (dst, mids[0], mids[-1])
    return routes


def _engines(mask):
    return bin(mask).count("1")


def _halves(mask):
    bits = [1 << i for i in range(16) if (mask >> i) & 1]
    k = len(bits) // 2
    return sum(bits[:k]), sum(bits[k:])


def rank_program(g, core, T, topo):
    if T.rank_of(core) is None:
        return
    S = T.sem
    routes = _routes(T, topo)
    sent = [0]

    def cols(buf, h):
        return buf[:, h * H:h * H + H]

    def codes(h, src_buf, dst, last):
        rid, pid = topo.addr(dst, core)
        mask = topo.mask(core, dst)
        g.remote_dma(out_ap=cols(T.lq if last else T.rq, h).bitcast(dt.uint8), in_ap=cols(src_buf, h).bitcast(dt.uint8),
                     remote_sem=S["arr%d" % h] if last else S["inq%d" % h], local_sem=S.sent, pid=pid, routing_id=rid,
                     dma_engine_mask=mask)
        sent[0] += _engines(mask)

    def plane(src_buf, dst, last):
        rid, pid = topo.addr(dst, core)
        masks = _halves(topo.mask(core, dst))
        g.remote_dma_fused([RemoteDMATransfer(dst_ids=[DstId(rid=rid, pnc=pid)], dma_engine_mask=masks[h],
                                              remote_sem=S["arr%d" % h] if last else S.ins,
                                              src=cols(src_buf, h), dst=cols(T.ls if last else T.rs, h))
                            for h in (0, 1)], local_sem=S.sent)
        sent[0] += _engines(masks[0]) + _engines(masks[1])

    for h in (0, 1):
        g.sync.dma_start(T.xb[:, 4 * h * H:4 * (h + 1) * H], T.x[:, 4 * h * H:4 * (h + 1) * H]).then_inc(S["ld%d" % h], 16)
    g.sync.dma_start(T.wb[:], T.w[:]).then_inc(S.ldw, 16)
    for h in (0, 1):
        g.vector.wait_ge(S["ld%d" % h], 16)
        g.vector.quantize_mx(cols(T.xq, h), cols(T.xs, h), T.xb[:, 4 * h * H:4 * (h + 1) * H]).then_inc(S["q%d" % h], 1)
    g.vector.wait_ge(S.ldw, 16)
    g.vector.quantize_mx(T.wq[:], T.ws[:], T.wb[:]).then_inc(S.qw, 1)

    end, to_q, to_s = routes[core]
    for h in (0, 1):
        g.wait_ge(S["q%d" % h], 1)
        codes(h, T.xq, to_q, to_q == end)
    plane(T.xs, to_s, to_s == end)

    arrive = [0, 0]
    for src, (dst, mid_q, mid_s) in routes.items():
        if mid_q == core and dst != core:
            for h in (0, 1):
                g.wait_ge(S["inq%d" % h], _engines(topo.mask(src, core)))
                codes(h, T.rq, dst, True)
        if mid_s == core and dst != core:
            g.wait_ge(S.ins, _engines(topo.mask(src, core)))
            plane(T.rs, dst, True)
        if dst == core:
            for h in (0, 1):
                arrive[h] = (_engines(topo.mask(src if mid_q == dst else mid_q, core))
                             + _engines(_halves(topo.mask(src if mid_s == dst else mid_s, core))[h]))

    g.tensor.wait_ge(S.qw, 1)
    for h in (0, 1):
        g.tensor.wait_ge(S["arr%d" % h], arrive[h])
        g.tensor.matmul_mx(T.ps[:, 512 * h:512 * h + H], T.wq[:], T.ws[:], cols(T.lq, h), cols(T.ls, h),
                           True, True).then_inc(S["mm%d" % h], 1)
    g.vector.wait_ge(S.mm0, 1)
    g.vector.tensor_copy(cols(T.yb, 0), T.ps[:, 0:H]).then_inc(S.cp0, 1)
    g.scalar.wait_ge(S.mm1, 1)
    g.scalar.activation(cols(T.yb, 1), T.ps[:, 512:512 + H], ActivationFunctionType.Copy).then_inc(S.cp1, 1)
    for h in (0, 1):
        g.sync.wait_ge(S["cp%d" % h], 1)
        g.sync.dma_start(cols(T.y, h), cols(T.yb, h)).then_inc(S.st, 16)
    g.sync.wait_ge(S.st, 32)
    g.wait_ge(S.sent, sent[0])
